import numpy as np
import ml_dtypes


def mxq(x, axis, fmt="e4m3"):
    dtype, down = {"e4m3": (ml_dtypes.float8_e4m3fn, 7), "e5m2": (ml_dtypes.float8_e5m2, 14)}[fmt]
    v = np.moveaxis(np.asarray(x, np.float32).astype(ml_dtypes.bfloat16).astype(np.float64), axis, -1)
    blocks = v.reshape(v.shape[:-1] + (-1, 32))
    amax = np.abs(blocks).max(-1, keepdims=True)
    byte = np.maximum(np.where(amax > 0, np.frexp(amax)[1] - 1 + 127, 0) - down, 1)
    scale = np.exp2(byte - 127.0)
    codes = (blocks / scale).astype(np.float32).astype(dtype).astype(np.float64)
    return np.moveaxis((codes * scale).reshape(v.shape), -1, axis)


WIDE = False


def mx_kscale(k):
    if not WIDE:
        return np.ones(k)
    levels = np.array([10, -10, 5, -5, 0])
    if k % 512:
        return np.exp2(np.random.permutation(np.resize(levels, k // 32))).repeat(32)
    a = np.empty((k // 512, 16))
    for p in range(k // 512):
        a[p, :8] = np.random.permutation(np.resize(levels, 8))
        for g in range(8):
            far = levels[np.abs(levels - a[p, g]) >= 10]
            a[p, g + 8] = far[np.random.randint(len(far))]
    return np.exp2(a.ravel()).repeat(32)


def f64(x):
    return np.asarray(x).astype(np.float64)


def striped(idx):
    return np.tile(idx.reshape(-1, 16).T, (8, 1)).astype(np.uint16)


def unstriped(offs):
    return offs[:16].T.reshape(-1).astype(np.int64)


E2M1 = np.array([0.0, 0.5, 1.0, 1.5, 2.0, 3.0, 4.0, 6.0, -0.0, -0.5, -1.0, -1.5, -2.0, -3.0, -4.0, -6.0])


def pack_weight(w, fmt):
    k, n = w.shape
    w = f64(np.asarray(w, np.float32).astype(ml_dtypes.bfloat16)).reshape(k // 32, 32, n)
    amax = np.abs(w).max(1)
    if fmt == "e4m3":
        byte = np.frexp(amax)[1] - 1 + 127 - 7
    else:
        mant, ex = np.frexp(amax / 6.0)
        byte = np.where(mant > 0.5, ex, ex - 1) + 127
    byte = np.clip(np.where(amax > 0, byte, 1), 1, 254)
    scaled = (w * np.exp2(127.0 - byte)[:, None, :]).reshape(k, n).astype(np.float32)
    by_word = np.ascontiguousarray(scaled.reshape(k // 512, 128, 4, n).transpose(0, 1, 3, 2))
    if fmt == "e4m3":
        words = by_word.astype(ml_dtypes.float8_e4m3fn).view(np.uint8)
    else:
        c = by_word.astype(ml_dtypes.float4_e2m1fn).view(np.uint8) & 0xF
        words = (c[..., 0::2] | (c[..., 1::2] << 4)).reshape(k // 512, 128, 2 * n)
    return np.ascontiguousarray(words), np.ascontiguousarray(byte.astype(np.uint8).reshape(k // 512, 16, n))


def unpack_weight(words, scales, fmt):
    g, _, n = scales.shape
    words = np.ascontiguousarray(words).reshape(g, 128, n, -1)
    if fmt == "e4m3":
        vals = words.view(ml_dtypes.float8_e4m3fn).astype(np.float64)
    else:
        nib = np.empty((g, 128, n, 4), np.uint8)
        nib[..., 0::2] = words & 0xF
        nib[..., 1::2] = words >> 4
        vals = E2M1[nib]
    vals = vals * np.repeat(np.exp2(scales.astype(np.float64) - 127.0), 8, axis=1)[..., None]
    return vals.transpose(0, 1, 3, 2).reshape(g * 512, n)


def sigmoid(v):
    return 1.0 / (1.0 + np.exp(-np.maximum(v, -700.0)))


def d_sigmoid(v):
    s = 1.0 / (1.0 + np.exp(-np.maximum(v, -700.0)))
    return s * (1.0 - s)


K, T, E, C, H, N = 256, 640, 2, 256, 512, 1024


def by_expert(wq, xq):
    return np.concatenate([wq[e].T @ xq[:, e * C:(e + 1) * C] for e in range(E)], axis=1)


def setup_inputs():
    n = np.random.standard_normal
    s = mx_kscale(N)[:, None]
    u = mx_kscale(H)
    w2 = [pack_weight(m, "e2m1") for m in n((E, N, H)) / np.sqrt(N) / s[None] * u[None, None, :]]
    w1 = [pack_weight(m, "e2m1") for m in n((E, H, K)) / np.sqrt(H) / u[None, :, None]]
    w3 = [pack_weight(m, "e2m1") for m in n((E, H, K)) / np.sqrt(H) / u[None, :, None]]
    return {
        "dyT": (n((N, T)) * s).astype(np.float32),
        "a1": n((H, E * C)).astype(np.float32),
        "a3": n((H, E * C)).astype(np.float32),
        "w2_words": np.stack([m[0] for m in w2]),
        "w2_scales": np.stack([m[1] for m in w2]),
        "w1_words": np.stack([m[0] for m in w1]),
        "w1_scales": np.stack([m[1] for m in w1]),
        "w3_words": np.stack([m[0] for m in w3]),
        "w3_scales": np.stack([m[1] for m in w3]),
        "gate": np.tile(np.random.uniform(0.2, 1.0, E * C), (N, 1)).astype(np.float32),
        "offs": striped(np.random.permutation(T)[:E * C]),
    }


def reference(dyT, a1, a3, w2_words, w2_scales, w1_words, w1_scales, w3_words, w3_scales, gate, offs):
    idx = unstriped(offs)
    w2 = np.stack([unpack_weight(w2_words[e], w2_scales[e], "e2m1") for e in range(E)])
    w1 = np.stack([unpack_weight(w1_words[e], w1_scales[e], "e2m1") for e in range(E)])
    w3 = np.stack([unpack_weight(w3_words[e], w3_scales[e], "e2m1") for e in range(E)])
    gq = mxq(f64(gate) * f64(dyT)[:, idx], 0, "e4m3")
    dh = by_expert(w2, gq)
    da1 = dh * f64(a3) * d_sigmoid(f64(a1))
    da3 = dh * sigmoid(f64(a1))
    dx = by_expert(w1, mxq(da1, 0, "e4m3")) + by_expert(w3, mxq(da3, 0, "e4m3"))
    out = np.zeros((K, T))
    out[:, idx] = dx
    return out

@@ -1,0 +1,265 @@
+from contextlib import ExitStack
+
+import concourse.mybir as mybir
+from concourse.masks import make_identity
+
+N, H, K, T, E, C = 1024, 512, 256, 640, 2, 256
+P = 128
+PACK = 4
+SLOTS = E * C
+PASSES = N // (P * PACK)
+HALF = 128
+
+FLOPS = 805306368
+BYTES = 4 * (N * T + 2 * H * SLOTS + SLOTS + K * T) + E * N * H // 2 + 2 * E * H * K // 2 + E * (N * H + 2 * H * K) // 32 + 2 * SLOTS
+
+F32 = mybir.dt.float32
+BF16 = mybir.dt.bfloat16
+I32 = mybir.dt.int32
+U32 = mybir.dt.uint32
+U16 = mybir.dt.uint16
+U8 = mybir.dt.uint8
+FP8X4 = mybir.dt.float8_e4m3fn_x4
+FP4X4 = mybir.dt.float4_e2m1fn_x4
+MULT = mybir.AluOpType.mult
+SIGMOID = mybir.ActivationFunctionType.Sigmoid
+
+
+def tile_moe_bdx_glu_sigmoid_kernel(tc, dyT, a1, a3, w2_words, w2_scales, w1_words, w1_scales, w3_words, w3_scales, gate, offs, out):
+    nc = tc.nc
+    with ExitStack() as ctx:
+        keep = ctx.enter_context(tc.tile_pool(name="keep", bufs=1))
+        raw_pool = ctx.enter_context(tc.psum_pool(name="raw_pool", bufs=2))
+        turn_pool = ctx.enter_context(tc.psum_pool(name="turn_pool", bufs=4))
+        dx_pool = ctx.enter_context(tc.psum_pool(name="dx_pool", bufs=2))
+
+        offsets = keep.tile([P, SLOTS // 16], U16, name="offsets")
+        gate_sb = keep.tile([P, SLOTS], F32, name="gate_sb")
+        dy = [[keep.tile([P, T], F32, name=f"dy{s}{j}") for j in range(PACK)] for s in range(PASSES)]
+        a1_sb = [keep.tile([P, PACK, C], F32, name=f"a1_sb{e}") for e in range(E)]
+        a3_sb = [keep.tile([P, PACK, C], F32, name=f"a3_sb{e}") for e in range(E)]
+        w2_sb = keep.tile([P, E, PASSES, 2 * H], U8, name="w2_sb", align_bytes=64)
+        w1_sb = keep.tile([P, E, 2 * K], U8, name="w1_sb", align_bytes=64)
+        w3_sb = keep.tile([P, E, 2 * K], U8, name="w3_sb", align_bytes=64)
+        w2_sc = keep.tile([P, E, PASSES, H], U8, name="w2_sc", align_bytes=64)
+        w1_sc = keep.tile([P, E, K], U8, name="w1_sc", align_bytes=64)
+        w3_sc = keep.tile([P, E, K], U8, name="w3_sc", align_bytes=64)
+        ident = keep.tile([P, P], F32, name="ident")
+        warm = keep.tile([P, 1], F32, name="warm")
+        out_sb = [keep.tile([P, T], F32, name=f"out_sb{k}") for k in range(K // P)]
+
+        dy_rows = dyT.rearrange("(s p j) t -> s j p t", p=P, j=PACK)
+        a1_rows = a1.rearrange("(p t) n -> p t n", t=PACK)
+        a3_rows = a3.rearrange("(p t) n -> p t n", t=PACK)
+
+        def load_a(rows, tiles, e):
+            nc.sync.dma_start(out=tiles[e][:], in_=rows[:, :, e * C : (e + 1) * C])
+
+        nc.sync.dma_start(out=offsets[:], in_=offs)
+        def load_dy(s, j):
+            nc.sync.dma_start(out=dy[s][j][:], in_=dy_rows[s, j])
+
+        def load_w2(e):
+            nc.sync.dma_start(out=w2_sb[:, e].bitcast(I32), in_=w2_words[e].bitcast(I32).rearrange("s p b -> p s b"))
+
+        nc.sync.dma_start(out=gate_sb[:, 0:C], in_=gate[0:P, 0:C])
+        load_dy(0, 0)
+        nc.sync.dma_start(out=gate_sb[:, C:SLOTS], in_=gate[0:P, C:SLOTS])
+        for j in range(1, PACK):
+            load_dy(0, j)
+        load_a(a1_rows, a1_sb, 0)
+        for j in range(PACK):
+            load_dy(1, j)
+        load_w2(0)
+        load_a(a3_rows, a3_sb, 0)
+        load_w2(1)
+        for words, tile_sb in ((w1_words, w1_sb), (w3_words, w3_sb)):
+            nc.sync.dma_start(out=tile_sb[:].bitcast(I32), in_=words.bitcast(I32).rearrange("e s p b -> p (e s) b"))
+        load_a(a3_rows, a3_sb, 1)
+        load_a(a1_rows, a1_sb, 1)
+
+        nc.vector.memset(warm[:], 0.0)
+        nc.scalar.activation(warm[:], warm[:], SIGMOID)
+        nc.vector.memset(w2_sc[:].rearrange("p e s i -> p (e s i)").bitcast(I32), 0)
+        nc.vector.memset(w1_sc[:].rearrange("p e i -> p (e i)").bitcast(I32), 0)
+        nc.vector.memset(w3_sc[:].rearrange("p e i -> p (e i)").bitcast(I32), 0)
+        for r in range(4):
+            nc.scalar.dma_start(
+                out=w2_sc[:].rearrange("p e s i -> p (e s) i").bitcast(I32)[r:P:32],
+                in_=w2_scales.bitcast(I32).rearrange("e s (q r) i -> r q (e s) i", r=4)[r],
+            )
+        for scales, plane in ((w1_scales, w1_sc), (w3_scales, w3_sc)):
+            for r in range(4):
+                nc.sync.dma_start(
+                    out=plane[:].bitcast(I32)[r:P:32],
+                    in_=scales.bitcast(I32).rearrange("e s (q r) i -> r q (e s) i", r=4)[r],
+                )
+        make_identity(nc, ident[:])
+        for k in range(K // P):
+            nc.vector.memset(out_sb[k][:], 0.0)
+
+        g_bf = {}
+        g_codes = [[keep.tile([P, C], U32, name=f"g_codes{s}{e}", align_bytes=64) for e in range(E)] for s in range(PASSES)]
+        g_sc = [[keep.tile([P, C], U8, name=f"g_sc{s}{e}", align_bytes=64) for e in range(E)] for s in range(PASSES)]
+        sig = [keep.tile([P, PACK, C], F32, name=f"sig{e}") for e in range(E)]
+        neg = [keep.tile([P, PACK, C], F32, name=f"neg{e}") for e in range(E)]
+        rest = [keep.tile([P, PACK, C], F32, name=f"rest{e}") for e in range(E)]
+        dh = [[keep.tile([P, PACK, P], F32, name=f"dh{e}{h}") for h in range(2)] for e in range(E)]
+        da3_f = {}
+        da1_bf = [keep.tile([P, C, PACK], BF16, name=f"da1_bf{e}", align_bytes=64) for e in range(E)]
+        da3_bf = [keep.tile([P, C, PACK], BF16, name=f"da3_bf{e}", align_bytes=64) for e in range(E)]
+        da1_codes = [keep.tile([P, C], U32, name=f"da1_codes{e}", align_bytes=64) for e in range(E)]
+        da3_codes = [keep.tile([P, C], U32, name=f"da3_codes{e}", align_bytes=64) for e in range(E)]
+        da1_sc = [keep.tile([P, C], U8, name=f"da1_sc{e}", align_bytes=64) for e in range(E)]
+        da3_sc = [keep.tile([P, C], U8, name=f"da3_sc{e}", align_bytes=64) for e in range(E)]
+        dx_sb = {}
+        dx_bank = {}
+
+        g0 = keep.tile([P, PACK, SLOTS], F32, name="g0")
+        g1 = {}
+
+        def gather(out_ap, s, j, lo, hi):
+            nc.vector.tensor_tensor(out_ap, dy[s][j][:].indirect(offsets[:, lo // 16 : hi // 16]), gate_sb[:, lo:hi], MULT)
+
+        def gathers0():
+            gather(g0[:, 0, 0:C], 0, 0, 0, C)
+            gather(g0[:, 0, C:SLOTS], 0, 0, C, SLOTS)
+            for j in range(1, PACK):
+                gather(g0[:, j, :], 0, j, 0, SLOTS)
+
+        def gathers1(e):
+            g1[e] = keep.tile([P, PACK, C], F32, name="g1")
+            for j in range(PACK):
+                gather(g1[e][:, j, :], 1, j, e * C, (e + 1) * C)
+
+        def interleave(s, e):
+            g_bf[s, e] = keep.tile([P, C, PACK], BF16, name=f"g_bf{s}{e}", align_bytes=64)
+            source = g0[:, :, e * C : (e + 1) * C] if s == 0 else g1[e][:]
+            nc.scalar.copy(out=g_bf[s, e][:], in_=source.rearrange("p j n -> p n j"))
+
+        def quantize(values, codes, scales):
+            nc.vector.quantize_mx(out=codes[:].bitcast(FP8X4), scales=scales[:], in_=values[:].rearrange("p n j -> p (n j)"))
+
+        def sigmoid(e):
+            nc.scalar.activation(sig[e][:], a1_sb[e][:], SIGMOID)
+
+        def complement(e):
+            nc.scalar.activation(neg[e][:], a1_sb[e][:], SIGMOID, scale=-1.0)
+
+        def factor(e):
+            nc.vector.tensor_tensor(rest[e][:], neg[e][:], a3_sb[e][:], MULT)
+
+        raw = {}
+
+        def first_product(e, s):
+            for h in range(2):
+                if s == 0:
+                    raw[e, h] = raw_pool.tile([P, H], F32, name="raw_bank")
+                cols = slice(h * HALF, (h + 1) * HALF)
+                nc.tensor.matmul_mx(
+                    out=raw[e, h][:],
+                    lhsT=g_codes[s][e][:, cols].bitcast(FP8X4),
+                    lhsT_scale=g_sc[s][e][:, cols],
+                    rhs=w2_sb[:, e, s, :].bitcast(FP4X4),
+                    rhs_scale=w2_sc[:, e, s, :],
+                    start=(s == 0),
+                    stop=(s == PASSES - 1),
+                )
+
+        turned = {}
+
+        def turn(e):
+            for h in range(2):
+                nc.scalar.copy(out=dh[e][h][:], in_=raw[e, h][:].rearrange("p (m t) -> p t m", t=PACK))
+            for h in range(2):
+                turned[e, h] = turn_pool.tile([P, PACK, HALF], F32, name="turn_bank")
+                for t in range(PACK):
+                    nc.tensor.transpose(turned[e, h][:, t, :], dh[e][h][:, t, :], ident[:])
+
+        def grad3(e):
+            for h in range(2):
+                cols = slice(h * HALF, (h + 1) * HALF)
+                da3_f[e, h] = keep.tile([P, PACK, HALF], F32, name="g_bf11" if (e, h) == (0, 0) else f"da3_f{e}{h}", align_bytes=64)
+                nc.vector.tensor_tensor(da3_f[e, h][:], turned[e, h][:], sig[e][:, :, cols], MULT)
+
+        def round3(e):
+            for h in range(2):
+                cols = slice(h * HALF, (h + 1) * HALF)
+                nc.scalar.copy(out=da3_bf[e][:, cols, :], in_=da3_f[e, h][:].rearrange("p t n -> p n t"))
+
+        def grad1(e, engines):
+            for h, engine in enumerate(engines):
+                cols = slice(h * HALF, (h + 1) * HALF)
+                engine.tensor_tensor(
+                    da1_bf[e][:, cols, :],
+                    da3_f[e, h][:].rearrange("p t n -> p n t"),
+                    rest[e][:, :, cols].rearrange("p t n -> p n t"),
+                    MULT,
+                )
+
+        def second_product(e):
+            dx_bank[e] = dx_pool.tile([P, K // P, C], F32, name="dx_bank")
+            for k in range(K // P):
+                for h in range(2):
+                    cols = slice(h * HALF, (h + 1) * HALF)
+                    for words, w_sc, codes, scales in ((w3_sb, w3_sc, da3_codes, da3_sc), (w1_sb, w1_sc, da1_codes, da1_sc)):
+                        nc.tensor.matmul_mx(
+                            out=dx_bank[e][:, k, cols],
+                            lhsT=words[:, e, 2 * k * P : 2 * (k + 1) * P].bitcast(FP4X4),
+                            lhsT_scale=w_sc[:, e, k * P : (k + 1) * P],
+                            rhs=codes[e][:, cols].bitcast(FP8X4),
+                            rhs_scale=scales[e][:, cols],
+                            start=(words is w3_sb),
+                            stop=(words is w1_sb),
+                        )
+
+        def empty(e, k):
+            dx_sb[e, k] = keep.tile([P, C], F32, name="da3_f10" if (e, k) == (0, 1) else f"dx_sb{e}{k}", align_bytes=64)
+            nc.scalar.copy(out=dx_sb[e, k][:], in_=dx_bank[e][:, k, :])
+
+        def scatter(e, k):
+            nc.vector.tensor_copy(out_sb[k][:].indirect(offsets[:, e * C // 16 : (e + 1) * C // 16]), dx_sb[e, k][:])
+
+        gathers0()
+        complement(0)
+        sigmoid(0)
+        interleave(0, 0)
+        quantize(g_bf[0, 0], g_codes[0][0], g_sc[0][0])
+        first_product(0, 0)
+        gathers1(0)
+        interleave(1, 0)
+        interleave(0, 1)
+        quantize(g_bf[1, 0], g_codes[1][0], g_sc[1][0])
+        first_product(0, 1)
+        quantize(g_bf[0, 1], g_codes[0][1], g_sc[0][1])
+        gathers1(1)
+        turn(0)
+        interleave(1, 1)
+        factor(0)
+        quantize(g_bf[1, 1], g_codes[1][1], g_sc[1][1])
+        first_product(1, 0)
+        first_product(1, 1)
+        grad3(0)
+        grad1(0, (nc.gpsimd, nc.vector))
+        round3(0)
+        turn(1)
+        complement(1)
+        sigmoid(1)
+        quantize(da3_bf[0], da3_codes[0], da3_sc[0])
+        quantize(da1_bf[0], da1_codes[0], da1_sc[0])
+        second_product(0)
+        empty(0, 0)
+        factor(1)
+        grad3(1)
+        grad1(1, (nc.gpsimd, nc.vector))
+        round3(1)
+        scatter(0, 0)
+        quantize(da3_bf[1], da3_codes[1], da3_sc[1])
+        quantize(da1_bf[1], da1_codes[1], da1_sc[1])
+        second_product(1)
+        empty(0, 1)
+        scatter(0, 1)
+        for k in range(K // P):
+            empty(1, k)
+            scatter(1, k)
+            nc.sync.dma_start(out=out[k * P : (k + 1) * P, :], in_=out_sb[k][:])

@@ -22,15 +22,17 @@ U8 = mybir.dt.uint8
 FP8X4 = mybir.dt.float8_e4m3fn_x4
 FP4X4 = mybir.dt.float4_e2m1fn_x4
 MULT = mybir.AluOpType.mult
+SUBTRACT = mybir.AluOpType.subtract
 SIGMOID = mybir.ActivationFunctionType.Sigmoid
+COPY = mybir.ActivationFunctionType.Copy
 
 
 def tile_moe_bdx_glu_sigmoid_kernel(tc, dyT, a1, a3, w2_words, w2_scales, w1_words, w1_scales, w3_words, w3_scales, gate, offs, out):
     nc = tc.nc
     with ExitStack() as ctx:
         keep = ctx.enter_context(tc.tile_pool(name="keep", bufs=1))
-        raw_pool = ctx.enter_context(tc.psum_pool(name="raw_pool", bufs=2))
-        turn_pool = ctx.enter_context(tc.psum_pool(name="turn_pool", bufs=4))
+        raw_pool = ctx.enter_context(tc.psum_pool(name="raw_pool", bufs=4))
+        turn_pool = ctx.enter_context(tc.psum_pool(name="turn_pool", bufs=2))
         dx_pool = ctx.enter_context(tc.psum_pool(name="dx_pool", bufs=2))
 
         offsets = keep.tile([P, SLOTS // 16], U16, name="offsets")
@@ -59,24 +61,19 @@ def tile_moe_bdx_glu_sigmoid_kernel(tc, dyT, a1, a3, w2_words, w2_scales, w1_wor
         def load_dy(s, j):
             nc.sync.dma_start(out=dy[s][j][:], in_=dy_rows[s, j])
 
-        def load_w2(e):
-            nc.sync.dma_start(out=w2_sb[:, e].bitcast(I32), in_=w2_words[e].bitcast(I32).rearrange("s p b -> p s b"))
-
-        nc.sync.dma_start(out=gate_sb[:, 0:C], in_=gate[0:P, 0:C])
-        load_dy(0, 0)
-        nc.sync.dma_start(out=gate_sb[:, C:SLOTS], in_=gate[0:P, C:SLOTS])
-        for j in range(1, PACK):
+        nc.sync.dma_start(out=gate_sb[:], in_=gate[0:P, :])
+        for j in range(PACK):
             load_dy(0, j)
         load_a(a1_rows, a1_sb, 0)
         for j in range(PACK):
             load_dy(1, j)
-        load_w2(0)
+        for e in range(E):
+            nc.sync.dma_start(out=w2_sb[:, e].bitcast(I32), in_=w2_words[e].bitcast(I32).rearrange("s p b -> p s b"))
         load_a(a3_rows, a3_sb, 0)
-        load_w2(1)
+        load_a(a1_rows, a1_sb, 1)
+        load_a(a3_rows, a3_sb, 1)
         for words, tile_sb in ((w1_words, w1_sb), (w3_words, w3_sb)):
             nc.sync.dma_start(out=tile_sb[:].bitcast(I32), in_=words.bitcast(I32).rearrange("e s p b -> p (e s) b"))
-        load_a(a3_rows, a3_sb, 1)
-        load_a(a1_rows, a1_sb, 1)
 
         nc.vector.memset(warm[:], 0.0)
         nc.scalar.activation(warm[:], warm[:], SIGMOID)
@@ -98,75 +95,64 @@ def tile_moe_bdx_glu_sigmoid_kernel(tc, dyT, a1, a3, w2_words, w2_scales, w1_wor
         for k in range(K // P):
             nc.vector.memset(out_sb[k][:], 0.0)
 
-        g_bf = {}
-        g_codes = [[keep.tile([P, C], U32, name=f"g_codes{s}{e}", align_bytes=64) for e in range(E)] for s in range(PASSES)]
-        g_sc = [[keep.tile([P, C], U8, name=f"g_sc{s}{e}", align_bytes=64) for e in range(E)] for s in range(PASSES)]
+        g = [keep.tile([P, PACK, SLOTS], F32, name=f"g{s}") for s in range(PASSES)]
+        g_bf = [keep.tile([P, SLOTS, PACK], BF16, name=f"g_bf{s}", align_bytes=64) for s in range(PASSES)]
+        g_codes = [keep.tile([P, SLOTS], U32, name=f"g_codes{s}", align_bytes=64) for s in range(PASSES)]
+        g_sc = [keep.tile([P, SLOTS], U8, name=f"g_sc{s}", align_bytes=64) for s in range(PASSES)]
         sig = [keep.tile([P, PACK, C], F32, name=f"sig{e}") for e in range(E)]
-        neg = [keep.tile([P, PACK, C], F32, name=f"neg{e}") for e in range(E)]
         rest = [keep.tile([P, PACK, C], F32, name=f"rest{e}") for e in range(E)]
         dh = [[keep.tile([P, PACK, P], F32, name=f"dh{e}{h}") for h in range(2)] for e in range(E)]
-        da3_f = {}
-        da1_bf = [keep.tile([P, C, PACK], BF16, name=f"da1_bf{e}", align_bytes=64) for e in range(E)]
-        da3_bf = [keep.tile([P, C, PACK], BF16, name=f"da3_bf{e}", align_bytes=64) for e in range(E)]
-        da1_codes = [keep.tile([P, C], U32, name=f"da1_codes{e}", align_bytes=64) for e in range(E)]
-        da3_codes = [keep.tile([P, C], U32, name=f"da3_codes{e}", align_bytes=64) for e in range(E)]
-        da1_sc = [keep.tile([P, C], U8, name=f"da1_sc{e}", align_bytes=64) for e in range(E)]
-        da3_sc = [keep.tile([P, C], U8, name=f"da3_sc{e}", align_bytes=64) for e in range(E)]
+        da3_f = [[keep.tile([P, PACK, HALF], F32, name=f"da3_f{e}{h}", align_bytes=64) for h in range(2)] for e in range(E)]
+        da_bf = [keep.tile([P, 2, C, PACK], BF16, name=f"da_bf{e}", align_bytes=64) for e in range(E)]
+        da_codes = [keep.tile([P, 2, C], U32, name=f"da_codes{e}", align_bytes=64) for e in range(E)]
+        da_sc = [keep.tile([P, 2, C], U8, name=f"da_sc{e}", align_bytes=64) for e in range(E)]
         dx_sb = {}
+        raw = {}
+        turned = {}
         dx_bank = {}
 
-        g0 = keep.tile([P, PACK, SLOTS], F32, name="g0")
-        g1 = {}
-
-        def gather(out_ap, s, j, lo, hi):
-            nc.vector.tensor_tensor(out_ap, dy[s][j][:].indirect(offsets[:, lo // 16 : hi // 16]), gate_sb[:, lo:hi], MULT)
-
-        def gathers0():
-            gather(g0[:, 0, 0:C], 0, 0, 0, C)
-            gather(g0[:, 0, C:SLOTS], 0, 0, C, SLOTS)
-            for j in range(1, PACK):
-                gather(g0[:, j, :], 0, j, 0, SLOTS)
-
-        def gathers1(e):
-            g1[e] = keep.tile([P, PACK, C], F32, name="g1")
+        def gathers(s):
             for j in range(PACK):
-                gather(g1[e][:, j, :], 1, j, e * C, (e + 1) * C)
+                nc.vector.tensor_tensor(g[s][:, j, :], dy[s][j][:].indirect(offsets[:]), gate_sb[:], MULT)
 
         def interleave(s, e):
-            g_bf[s, e] = keep.tile([P, C, PACK], BF16, name=f"g_bf{s}{e}", align_bytes=64)
-            source = g0[:, :, e * C : (e + 1) * C] if s == 0 else g1[e][:]
-            nc.scalar.copy(out=g_bf[s, e][:], in_=source.rearrange("p j n -> p n j"))
+            cols = slice(e * C, (e + 1) * C)
+            nc.scalar.copy(out=g_bf[s][:, cols, :], in_=g[s][:, :, cols].rearrange("p j n -> p n j"))
 
-        def quantize(values, codes, scales):
-            nc.vector.quantize_mx(out=codes[:].bitcast(FP8X4), scales=scales[:], in_=values[:].rearrange("p n j -> p (n j)"))
+        def quantize_g(s, lo, hi):
+            nc.vector.quantize_mx(
+                out=g_codes[s][:, lo:hi].bitcast(FP8X4),
+                scales=g_sc[s][:, lo:hi],
+                in_=g_bf[s][:, lo:hi, :].rearrange("p n j -> p (n j)"),
+            )
+
+        def quantize_da(e):
+            nc.vector.quantize_mx(
+                out=da_codes[e][:].rearrange("p w n -> p (w n)").bitcast(FP8X4),
+                scales=da_sc[e][:].rearrange("p w n -> p (w n)"),
+                in_=da_bf[e][:].rearrange("p w n t -> p (w n t)"),
+            )
 
         def sigmoid(e):
             nc.scalar.activation(sig[e][:], a1_sb[e][:], SIGMOID)
 
-        def complement(e):
-            nc.scalar.activation(neg[e][:], a1_sb[e][:], SIGMOID, scale=-1.0)
-
         def factor(e):
-            nc.vector.tensor_tensor(rest[e][:], neg[e][:], a3_sb[e][:], MULT)
-
-        raw = {}
+            nc.vector.scalar_tensor_tensor(out=rest[e][:], in0=sig[e][:], scalar=1.0, in1=a3_sb[e][:], op0=SUBTRACT, op1=MULT)
 
         def first_product(e, s):
             for h in range(2):
                 if s == 0:
                     raw[e, h] = raw_pool.tile([P, H], F32, name="raw_bank")
-                cols = slice(h * HALF, (h + 1) * HALF)
+                cols = slice(e * C + h * HALF, e * C + (h + 1) * HALF)
                 nc.tensor.matmul_mx(
                     out=raw[e, h][:],
-                    lhsT=g_codes[s][e][:, cols].bitcast(FP8X4),
-                    lhsT_scale=g_sc[s][e][:, cols],
+                    lhsT=g_codes[s][:, cols].bitcast(FP8X4),
+                    lhsT_scale=g_sc[s][:, cols],
                     rhs=w2_sb[:, e, s, :].bitcast(FP4X4),
                     rhs_scale=w2_sc[:, e, s, :],
                     start=(s == 0),
                     stop=(s == PASSES - 1),
                 )
-
-        turned = {}
 
         def turn(e):
             for h in range(2):
@@ -176,89 +162,85 @@ def tile_moe_bdx_glu_sigmoid_kernel(tc, dyT, a1, a3, w2_words, w2_scales, w1_wor
                 for t in range(PACK):
                     nc.tensor.transpose(turned[e, h][:, t, :], dh[e][h][:, t, :], ident[:])
 
-        def grad3(e):
-            for h in range(2):
-                cols = slice(h * HALF, (h + 1) * HALF)
-                da3_f[e, h] = keep.tile([P, PACK, HALF], F32, name="g_bf11" if (e, h) == (0, 0) else f"da3_f{e}{h}", align_bytes=64)
-                nc.vector.tensor_tensor(da3_f[e, h][:], turned[e, h][:], sig[e][:, :, cols], MULT)
+        def grad3(e, h):
+            cols = slice(h * HALF, (h + 1) * HALF)
+            nc.vector.tensor_tensor(da3_f[e][h][:], turned[e, h][:], sig[e][:, :, cols], MULT)
 
-        def round3(e):
-            for h in range(2):
-                cols = slice(h * HALF, (h + 1) * HALF)
-                nc.scalar.copy(out=da3_bf[e][:, cols, :], in_=da3_f[e, h][:].rearrange("p t n -> p n t"))
+        def round3(e, h):
+            cols = slice(h * HALF, (h + 1) * HALF)
+            nc.scalar.activation(da_bf[e][:, 0, cols, :], da3_f[e][h][:].rearrange("p t n -> p n t"), COPY, scale=-1.0)
 
-        def grad1(e, engines):
-            for h, engine in enumerate(engines):
-                cols = slice(h * HALF, (h + 1) * HALF)
-                engine.tensor_tensor(
-                    da1_bf[e][:, cols, :],
-                    da3_f[e, h][:].rearrange("p t n -> p n t"),
-                    rest[e][:, :, cols].rearrange("p t n -> p n t"),
-                    MULT,
-                )
+        def grad1(engine, e, h):
+            cols = slice(h * HALF, (h + 1) * HALF)
+            engine.tensor_tensor(
+                da_bf[e][:, 1, cols, :],
+                da3_f[e][h][:].rearrange("p t n -> p n t"),
+                rest[e][:, :, cols].rearrange("p t n -> p n t"),
+                MULT,
+            )
 
         def second_product(e):
             dx_bank[e] = dx_pool.tile([P, K // P, C], F32, name="dx_bank")
             for k in range(K // P):
                 for h in range(2):
                     cols = slice(h * HALF, (h + 1) * HALF)
-                    for words, w_sc, codes, scales in ((w3_sb, w3_sc, da3_codes, da3_sc), (w1_sb, w1_sc, da1_codes, da1_sc)):
+                    for i, (words, w_sc) in enumerate(((w3_sb, w3_sc), (w1_sb, w1_sc))):
                         nc.tensor.matmul_mx(
                             out=dx_bank[e][:, k, cols],
                             lhsT=words[:, e, 2 * k * P : 2 * (k + 1) * P].bitcast(FP4X4),
                             lhsT_scale=w_sc[:, e, k * P : (k + 1) * P],
-                            rhs=codes[e][:, cols].bitcast(FP8X4),
-                            rhs_scale=scales[e][:, cols],
-                            start=(words is w3_sb),
-                            stop=(words is w1_sb),
+                            rhs=da_codes[e][:, i, cols].bitcast(FP8X4),
+                            rhs_scale=da_sc[e][:, i, cols],
+                            start=(i == 0),
+                            stop=(i == 1),
                         )
 
         def empty(e, k):
-            dx_sb[e, k] = keep.tile([P, C], F32, name="da3_f10" if (e, k) == (0, 1) else f"dx_sb{e}{k}", align_bytes=64)
-            nc.scalar.copy(out=dx_sb[e, k][:], in_=dx_bank[e][:, k, :])
+            dx_sb[e, k] = keep.tile([P, C], F32, name=f"dx_sb{e}{k}")
+            nc.scalar.activation(dx_sb[e, k][:], dx_bank[e][:, k, :], COPY, scale=-1.0)
 
         def scatter(e, k):
             nc.vector.tensor_copy(out_sb[k][:].indirect(offsets[:, e * C // 16 : (e + 1) * C // 16]), dx_sb[e, k][:])
 
-        gathers0()
-        complement(0)
+        gathers(0)
         sigmoid(0)
         interleave(0, 0)
-        quantize(g_bf[0, 0], g_codes[0][0], g_sc[0][0])
-        first_product(0, 0)
-        gathers1(0)
-        interleave(1, 0)
         interleave(0, 1)
-        quantize(g_bf[1, 0], g_codes[1][0], g_sc[1][0])
-        first_product(0, 1)
-        quantize(g_bf[0, 1], g_codes[0][1], g_sc[0][1])
-        gathers1(1)
-        turn(0)
-        interleave(1, 1)
-        factor(0)
-        quantize(g_bf[1, 1], g_codes[1][1], g_sc[1][1])
+        gathers(1)
+        quantize_g(0, 0, SLOTS)
+        first_product(0, 0)
         first_product(1, 0)
-        first_product(1, 1)
-        grad3(0)
-        grad1(0, (nc.gpsimd, nc.vector))
-        round3(0)
-        turn(1)
-        complement(1)
         sigmoid(1)
-        quantize(da3_bf[0], da3_codes[0], da3_sc[0])
-        quantize(da1_bf[0], da1_codes[0], da1_sc[0])
-        second_product(0)
-        empty(0, 0)
+        factor(0)
+        interleave(1, 0)
+        interleave(1, 1)
+        quantize_g(1, 0, C)
+        first_product(0, 1)
+        turn(0)
+        quantize_g(1, C, SLOTS)
+        first_product(1, 1)
         factor(1)
-        grad3(1)
-        grad1(1, (nc.gpsimd, nc.vector))
-        round3(1)
-        scatter(0, 0)
-        quantize(da3_bf[1], da3_codes[1], da3_sc[1])
-        quantize(da1_bf[1], da1_codes[1], da1_sc[1])
+        for h in range(2):
+            grad3(0, h)
+        grad1(nc.gpsimd, 0, 0)
+        turn(1)
+        for h in range(2):
+            round3(0, h)
+        for h in range(2):
+            grad3(1, h)
+        grad1(nc.gpsimd, 1, 0)
+        grad1(nc.vector, 0, 1)
+        quantize_da(0)
+        second_product(0)
+        for h in range(2):
+            round3(1, h)
+        grad1(nc.vector, 1, 1)
+        quantize_da(1)
+        for k in range(K // P):
+            empty(0, k)
         second_product(1)
-        empty(0, 1)
-        scatter(0, 1)
+        for k in range(K // P):
+            scatter(0, k)
         for k in range(K // P):
             empty(1, k)
             scatter(1, k)

@@ -38,8 +38,8 @@ def tile_moe_bdx_glu_sigmoid_kernel(tc, dyT, a1, a3, w2_words, w2_scales, w1_wor
         offsets = keep.tile([P, SLOTS // 16], U16, name="offsets")
         gate_sb = keep.tile([P, SLOTS], F32, name="gate_sb")
         dy = [[keep.tile([P, T], F32, name=f"dy{s}{j}") for j in range(PACK)] for s in range(PASSES)]
-        a1_sb = [keep.tile([P, PACK, C], F32, name=f"a1_sb{e}") for e in range(E)]
-        a3_sb = [keep.tile([P, PACK, C], F32, name=f"a3_sb{e}") for e in range(E)]
+        a1_sb = keep.tile([P, PACK, SLOTS], F32, name="a1_sb")
+        a3_sb = keep.tile([P, PACK, SLOTS], F32, name="a3_sb")
         w2_sb = keep.tile([P, E, PASSES, 2 * H], U8, name="w2_sb", align_bytes=64)
         w1_sb = keep.tile([P, E, 2 * K], U8, name="w1_sb", align_bytes=64)
         w3_sb = keep.tile([P, E, 2 * K], U8, name="w3_sb", align_bytes=64)
@@ -51,47 +51,44 @@ def tile_moe_bdx_glu_sigmoid_kernel(tc, dyT, a1, a3, w2_words, w2_scales, w1_wor
         out_sb = [keep.tile([P, T], F32, name=f"out_sb{k}") for k in range(K // P)]
 
         dy_rows = dyT.rearrange("(s p j) t -> s j p t", p=P, j=PACK)
-        a1_rows = a1.rearrange("(p t) n -> p t n", t=PACK)
-        a3_rows = a3.rearrange("(p t) n -> p t n", t=PACK)
 
-        def load_a(rows, tiles, e):
-            nc.sync.dma_start(out=tiles[e][:], in_=rows[:, :, e * C : (e + 1) * C])
-
-        nc.sync.dma_start(out=offsets[:], in_=offs)
         def load_dy(s, j):
             nc.sync.dma_start(out=dy[s][j][:], in_=dy_rows[s, j])
 
+        nc.sync.dma_start(out=offsets[:], in_=offs)
         nc.sync.dma_start(out=gate_sb[:], in_=gate[0:P, :])
         for j in range(PACK):
             load_dy(0, j)
-        load_a(a1_rows, a1_sb, 0)
-        for j in range(PACK):
-            load_dy(1, j)
-        for e in range(E):
-            nc.sync.dma_start(out=w2_sb[:, e].bitcast(I32), in_=w2_words[e].bitcast(I32).rearrange("s p b -> p s b"))
-        load_a(a3_rows, a3_sb, 0)
-        load_a(a1_rows, a1_sb, 1)
-        load_a(a3_rows, a3_sb, 1)
+        load_dy(1, 0)
+        load_dy(1, 1)
+        nc.sync.dma_start(out=a1_sb[:], in_=a1.rearrange("(p t) n -> p t n", t=PACK))
+        load_dy(1, 2)
+        load_dy(1, 3)
+        nc.sync.dma_start(out=a3_sb[:], in_=a3.rearrange("(p t) n -> p t n", t=PACK))
+        nc.sync.dma_start(
+            out=w2_sb[:].rearrange("p e s b -> p (e s) b").bitcast(I32),
+            in_=w2_words.bitcast(I32).rearrange("e s p b -> p (e s) b"),
+        )
         for words, tile_sb in ((w1_words, w1_sb), (w3_words, w3_sb)):
             nc.sync.dma_start(out=tile_sb[:].bitcast(I32), in_=words.bitcast(I32).rearrange("e s p b -> p (e s) b"))
 
+        make_identity(nc, ident[:])
         nc.vector.memset(warm[:], 0.0)
         nc.scalar.activation(warm[:], warm[:], SIGMOID)
         nc.vector.memset(w2_sc[:].rearrange("p e s i -> p (e s i)").bitcast(I32), 0)
         nc.vector.memset(w1_sc[:].rearrange("p e i -> p (e i)").bitcast(I32), 0)
         nc.vector.memset(w3_sc[:].rearrange("p e i -> p (e i)").bitcast(I32), 0)
         for r in range(4):
-            nc.scalar.dma_start(
+            nc.gpsimd.dma_start(
                 out=w2_sc[:].rearrange("p e s i -> p (e s) i").bitcast(I32)[r:P:32],
                 in_=w2_scales.bitcast(I32).rearrange("e s (q r) i -> r q (e s) i", r=4)[r],
             )
         for scales, plane in ((w1_scales, w1_sc), (w3_scales, w3_sc)):
             for r in range(4):
-                nc.sync.dma_start(
+                nc.gpsimd.dma_start(
                     out=plane[:].bitcast(I32)[r:P:32],
                     in_=scales.bitcast(I32).rearrange("e s (q r) i -> r q (e s) i", r=4)[r],
                 )
-        make_identity(nc, ident[:])
         for k in range(K // P):
             nc.vector.memset(out_sb[k][:], 0.0)
 
@@ -99,7 +96,7 @@ def tile_moe_bdx_glu_sigmoid_kernel(tc, dyT, a1, a3, w2_words, w2_scales, w1_wor
         g_bf = [keep.tile([P, SLOTS, PACK], BF16, name=f"g_bf{s}", align_bytes=64) for s in range(PASSES)]
         g_codes = [keep.tile([P, SLOTS], U32, name=f"g_codes{s}", align_bytes=64) for s in range(PASSES)]
         g_sc = [keep.tile([P, SLOTS], U8, name=f"g_sc{s}", align_bytes=64) for s in range(PASSES)]
-        sig = [keep.tile([P, PACK, C], F32, name=f"sig{e}") for e in range(E)]
+        sig = keep.tile([P, PACK, SLOTS], F32, name="sig")
         rest = [keep.tile([P, PACK, C], F32, name=f"rest{e}") for e in range(E)]
         dh = [[keep.tile([P, PACK, P], F32, name=f"dh{e}{h}") for h in range(2)] for e in range(E)]
         da3_f = [[keep.tile([P, PACK, HALF], F32, name=f"da3_f{e}{h}", align_bytes=64) for h in range(2)] for e in range(E)]
@@ -115,9 +112,14 @@ def tile_moe_bdx_glu_sigmoid_kernel(tc, dyT, a1, a3, w2_words, w2_scales, w1_wor
             for j in range(PACK):
                 nc.vector.tensor_tensor(g[s][:, j, :], dy[s][j][:].indirect(offsets[:]), gate_sb[:], MULT)
 
-        def interleave(s, e):
-            cols = slice(e * C, (e + 1) * C)
-            nc.scalar.copy(out=g_bf[s][:, cols, :], in_=g[s][:, :, cols].rearrange("p j n -> p n j"))
+        def side_by_side(ap):
+            return ap.rearrange("p (c i) t -> p c t i", i=4)
+
+        def apart(ap):
+            return ap.rearrange("p t (c i) -> p c t i", i=4)
+
+        def interleave(copy, s, e):
+            copy(out=side_by_side(g_bf[s][:, slots(e), :]), in_=apart(g[s][:, :, slots(e)]))
 
         def quantize_g(s, lo, hi):
             nc.vector.quantize_mx(
@@ -133,11 +135,14 @@ def tile_moe_bdx_glu_sigmoid_kernel(tc, dyT, a1, a3, w2_words, w2_scales, w1_wor
                 in_=da_bf[e][:].rearrange("p w n t -> p (w n t)"),
             )
 
+        def slots(e, h=None):
+            return slice(e * C, (e + 1) * C) if h is None else slice(e * C + h * HALF, e * C + (h + 1) * HALF)
+
         def sigmoid(e):
-            nc.scalar.activation(sig[e][:], a1_sb[e][:], SIGMOID)
+            nc.scalar.activation(sig[:, :, slots(e)], a1_sb[:, :, slots(e)], SIGMOID)
 
         def factor(e):
-            nc.vector.scalar_tensor_tensor(out=rest[e][:], in0=sig[e][:], scalar=1.0, in1=a3_sb[e][:], op0=SUBTRACT, op1=MULT)
+            nc.vector.scalar_tensor_tensor(out=rest[e][:], in0=sig[:, :, slots(e)], scalar=1.0, in1=a3_sb[:, :, slots(e)], op0=SUBTRACT, op1=MULT)
 
         def first_product(e, s):
             for h in range(2):
@@ -164,18 +169,18 @@ def tile_moe_bdx_glu_sigmoid_kernel(tc, dyT, a1, a3, w2_words, w2_scales, w1_wor
 
         def grad3(e, h):
             cols = slice(h * HALF, (h + 1) * HALF)
-            nc.vector.tensor_tensor(da3_f[e][h][:], turned[e, h][:], sig[e][:, :, cols], MULT)
+            nc.vector.tensor_tensor(da3_f[e][h][:], turned[e, h][:], sig[:, :, slots(e, h)], MULT)
 
         def round3(e, h):
             cols = slice(h * HALF, (h + 1) * HALF)
-            nc.scalar.activation(da_bf[e][:, 0, cols, :], da3_f[e][h][:].rearrange("p t n -> p n t"), COPY, scale=-1.0)
+            nc.scalar.activation(side_by_side(da_bf[e][:, 0, cols, :]), apart(da3_f[e][h][:]), COPY, scale=-1.0)
 
         def grad1(engine, e, h):
             cols = slice(h * HALF, (h + 1) * HALF)
             engine.tensor_tensor(
-                da_bf[e][:, 1, cols, :],
-                da3_f[e][h][:].rearrange("p t n -> p n t"),
-                rest[e][:, :, cols].rearrange("p t n -> p n t"),
+                side_by_side(da_bf[e][:, 1, cols, :]),
+                apart(da3_f[e][h][:]),
+                apart(rest[e][:, :, cols]),
                 MULT,
             )
 
@@ -204,18 +209,18 @@ def tile_moe_bdx_glu_sigmoid_kernel(tc, dyT, a1, a3, w2_words, w2_scales, w1_wor
 
         gathers(0)
         sigmoid(0)
-        interleave(0, 0)
-        interleave(0, 1)
+        interleave(nc.scalar.copy, 0, 0)
+        interleave(nc.scalar.copy, 0, 1)
         gathers(1)
+        interleave(nc.vector.tensor_copy, 1, 0)
         quantize_g(0, 0, SLOTS)
         first_product(0, 0)
-        first_product(1, 0)
         sigmoid(1)
-        factor(0)
-        interleave(1, 0)
-        interleave(1, 1)
+        interleave(nc.scalar.copy, 1, 1)
         quantize_g(1, 0, C)
         first_product(0, 1)
+        first_product(1, 0)
+        factor(0)
         turn(0)
         quantize_g(1, C, SLOTS)
         first_product(1, 1)

@@ -64,11 +64,11 @@ def tile_moe_bdx_glu_sigmoid_kernel(tc, dyT, a1, a3, w2_words, w2_scales, w1_wor
         nc.sync.dma_start(out=a1_sb[:], in_=a1.rearrange("(p t) n -> p t n", t=PACK))
         load_dy(1, 2)
         load_dy(1, 3)
-        nc.sync.dma_start(out=a3_sb[:], in_=a3.rearrange("(p t) n -> p t n", t=PACK))
         nc.sync.dma_start(
             out=w2_sb[:].rearrange("p e s b -> p (e s) b").bitcast(I32),
             in_=w2_words.bitcast(I32).rearrange("e s p b -> p (e s) b"),
         )
+        nc.sync.dma_start(out=a3_sb[:], in_=a3.rearrange("(p t) n -> p t n", t=PACK))
         for words, tile_sb in ((w1_words, w1_sb), (w3_words, w3_sb)):
             nc.sync.dma_start(out=tile_sb[:].bitcast(I32), in_=words.bitcast(I32).rearrange("e s p b -> p (e s) b"))
 
@@ -106,11 +106,12 @@ def tile_moe_bdx_glu_sigmoid_kernel(tc, dyT, a1, a3, w2_words, w2_scales, w1_wor
         dx_sb = {}
         raw = {}
         turned = {}
-        dx_bank = {}
 
-        def gathers(s):
-            for j in range(PACK):
-                nc.vector.tensor_tensor(g[s][:, j, :], dy[s][j][:].indirect(offsets[:]), gate_sb[:], MULT)
+        def gather(s, j, cols):
+            lists = offsets[:, cols.start // 16 : cols.stop // 16]
+            nc.vector.tensor_tensor(g[s][:, j, cols], dy[s][j][:].indirect(lists), gate_sb[:, cols], MULT)
+
+        everything = slice(0, SLOTS)
 
         def side_by_side(ap):
             return ap.rearrange("p (c i) t -> p c t i", i=4)
@@ -184,35 +185,36 @@ def tile_moe_bdx_glu_sigmoid_kernel(tc, dyT, a1, a3, w2_words, w2_scales, w1_wor
                 MULT,
             )
 
-        def second_product(e):
-            dx_bank[e] = dx_pool.tile([P, K // P, C], F32, name="dx_bank")
-            for k in range(K // P):
-                for h in range(2):
-                    cols = slice(h * HALF, (h + 1) * HALF)
-                    for i, (words, w_sc) in enumerate(((w3_sb, w3_sc), (w1_sb, w1_sc))):
-                        nc.tensor.matmul_mx(
-                            out=dx_bank[e][:, k, cols],
-                            lhsT=words[:, e, 2 * k * P : 2 * (k + 1) * P].bitcast(FP4X4),
-                            lhsT_scale=w_sc[:, e, k * P : (k + 1) * P],
-                            rhs=da_codes[e][:, i, cols].bitcast(FP8X4),
-                            rhs_scale=da_sc[e][:, i, cols],
-                            start=(i == 0),
-                            stop=(i == 1),
-                        )
-
-        def empty(e, k):
+        def second_product(e, k):
+            bank = dx_pool.tile([P, C], F32, name="dx_bank")
+            for h in range(2):
+                cols = slice(h * HALF, (h + 1) * HALF)
+                for i, (words, w_sc) in enumerate(((w3_sb, w3_sc), (w1_sb, w1_sc))):
+                    nc.tensor.matmul_mx(
+                        out=bank[:, cols],
+                        lhsT=words[:, e, 2 * k * P : 2 * (k + 1) * P].bitcast(FP4X4),
+                        lhsT_scale=w_sc[:, e, k * P : (k + 1) * P],
+                        rhs=da_codes[e][:, i, cols].bitcast(FP8X4),
+                        rhs_scale=da_sc[e][:, i, cols],
+                        start=(i == 0),
+                        stop=(i == 1),
+                    )
             dx_sb[e, k] = keep.tile([P, C], F32, name=f"dx_sb{e}{k}")
-            nc.scalar.activation(dx_sb[e, k][:], dx_bank[e][:, k, :], COPY, scale=-1.0)
+            nc.scalar.activation(dx_sb[e, k][:], bank[:], COPY, scale=-1.0)
 
         def scatter(e, k):
             nc.vector.tensor_copy(out_sb[k][:].indirect(offsets[:, e * C // 16 : (e + 1) * C // 16]), dx_sb[e, k][:])
 
-        gathers(0)
+        for j in range(PACK):
+            gather(0, j, everything)
         sigmoid(0)
         interleave(nc.scalar.copy, 0, 0)
         interleave(nc.scalar.copy, 0, 1)
-        gathers(1)
-        interleave(nc.vector.tensor_copy, 1, 0)
+        for j in range(PACK - 1):
+            gather(1, j, everything)
+        for e in range(E):
+            gather(1, PACK - 1, slots(e))
+        interleave(nc.scalar.copy, 1, 0)
         quantize_g(0, 0, SLOTS)
         first_product(0, 0)
         sigmoid(1)
@@ -225,28 +227,27 @@ def tile_moe_bdx_glu_sigmoid_kernel(tc, dyT, a1, a3, w2_words, w2_scales, w1_wor
         quantize_g(1, C, SLOTS)
         first_product(1, 1)
         factor(1)
-        for h in range(2):
-            grad3(0, h)
+        grad3(0, 0)
         grad1(nc.gpsimd, 0, 0)
+        grad3(0, 1)
+        grad1(nc.vector, 0, 1)
         turn(1)
         for h in range(2):
             round3(0, h)
-        for h in range(2):
-            grad3(1, h)
-        grad1(nc.gpsimd, 1, 0)
-        grad1(nc.vector, 0, 1)
         quantize_da(0)
-        second_product(0)
+        for k in range(K // P):
+            second_product(0, k)
+        grad3(1, 0)
+        grad1(nc.gpsimd, 1, 0)
+        grad3(1, 1)
+        grad1(nc.vector, 1, 1)
         for h in range(2):
             round3(1, h)
-        grad1(nc.vector, 1, 1)
         quantize_da(1)
-        for k in range(K // P):
-            empty(0, k)
-        second_product(1)
         for k in range(K // P):
             scatter(0, k)
         for k in range(K // P):
-            empty(1, k)
+            second_product(1, k)
+        for k in range(K // P):
             scatter(1, k)
             nc.sync.dma_start(out=out[k * P : (k + 1) * P, :], in_=out_sb[k][:])

@@ -162,7 +162,9 @@ def tile_moe_bdx_glu_sigmoid_kernel(tc, dyT, a1, a3, w2_words, w2_scales, w1_wor
 
         def turn(e):
             for h in range(2):
-                nc.scalar.copy(out=dh[e][h][:], in_=raw[e, h][:].rearrange("p (m t) -> p t m", t=PACK))
+                by_channel = raw[e, h][:].rearrange("p (m t) -> p t m", t=PACK)
+                for t in range(0, PACK, 2):
+                    nc.scalar.copy(out=dh[e][h][:, t : t + 2, :], in_=by_channel[:, t : t + 2, :])
             for h in range(2):
                 turned[e, h] = turn_pool.tile([P, PACK, HALF], F32, name="turn_bank")
                 for t in range(PACK):
@@ -215,8 +217,9 @@ def tile_moe_bdx_glu_sigmoid_kernel(tc, dyT, a1, a3, w2_words, w2_scales, w1_wor
         for e in range(E):
             gather(1, PACK - 1, slots(e))
         interleave(nc.scalar.copy, 1, 0)
-        quantize_g(0, 0, SLOTS)
+        quantize_g(0, 0, C)
         first_product(0, 0)
+        quantize_g(0, C, SLOTS)
         sigmoid(1)
         interleave(nc.scalar.copy, 1, 1)
         quantize_g(1, 0, C)

from contextlib import ExitStack

import concourse.mybir as mybir
from concourse.masks import make_identity

N, H, K, T, E, C = 1024, 512, 256, 640, 2, 256
P = 128
PACK = 4
SLOTS = E * C
PASSES = N // (P * PACK)
HALF = 128

FLOPS = 805306368
BYTES = 4 * (N * T + 2 * H * SLOTS + SLOTS + K * T) + E * N * H // 2 + 2 * E * H * K // 2 + E * (N * H + 2 * H * K) // 32 + 2 * SLOTS

F32 = mybir.dt.float32
BF16 = mybir.dt.bfloat16
I32 = mybir.dt.int32
U32 = mybir.dt.uint32
U16 = mybir.dt.uint16
U8 = mybir.dt.uint8
FP8X4 = mybir.dt.float8_e4m3fn_x4
FP4X4 = mybir.dt.float4_e2m1fn_x4
MULT = mybir.AluOpType.mult
SUBTRACT = mybir.AluOpType.subtract
SIGMOID = mybir.ActivationFunctionType.Sigmoid
COPY = mybir.ActivationFunctionType.Copy


def tile_moe_bdx_glu_sigmoid_kernel(tc, dyT, a1, a3, w2_words, w2_scales, w1_words, w1_scales, w3_words, w3_scales, gate, offs, out):
    nc = tc.nc
    with ExitStack() as ctx:
        keep = ctx.enter_context(tc.tile_pool(name="keep", bufs=1))
        raw_pool = ctx.enter_context(tc.psum_pool(name="raw_pool", bufs=4))
        turn_pool = ctx.enter_context(tc.psum_pool(name="turn_pool", bufs=2))
        dx_pool = ctx.enter_context(tc.psum_pool(name="dx_pool", bufs=2))

        offsets = keep.tile([P, SLOTS // 16], U16, name="offsets")
        gate_sb = keep.tile([P, SLOTS], F32, name="gate_sb")
        dy = [[keep.tile([P, T], F32, name=f"dy{s}{j}") for j in range(PACK)] for s in range(PASSES)]
        a1_sb = keep.tile([P, PACK, SLOTS], F32, name="a1_sb")
        a3_sb = keep.tile([P, PACK, SLOTS], F32, name="a3_sb")
        w2_sb = keep.tile([P, E, PASSES, 2 * H], U8, name="w2_sb", align_bytes=64)
        w1_sb = keep.tile([P, E, 2 * K], U8, name="w1_sb", align_bytes=64)
        w3_sb = keep.tile([P, E, 2 * K], U8, name="w3_sb", align_bytes=64)
        w2_sc = keep.tile([P, E, PASSES, H], U8, name="w2_sc", align_bytes=64)
        w1_sc = keep.tile([P, E, K], U8, name="w1_sc", align_bytes=64)
        w3_sc = keep.tile([P, E, K], U8, name="w3_sc", align_bytes=64)
        ident = keep.tile([P, P], F32, name="ident")
        warm = keep.tile([P, 1], F32, name="warm")
        out_sb = [keep.tile([P, T], F32, name=f"out_sb{k}") for k in range(K // P)]

        dy_rows = dyT.rearrange("(s p j) t -> s j p t", p=P, j=PACK)

        def load_dy(s, j):
            nc.sync.dma_start(out=dy[s][j][:], in_=dy_rows[s, j])

        nc.sync.dma_start(out=offsets[:], in_=offs)
        nc.sync.dma_start(out=gate_sb[:], in_=gate[0:P, :])
        for j in range(PACK):
            load_dy(0, j)
        load_dy(1, 0)
        load_dy(1, 1)
        nc.sync.dma_start(out=a1_sb[:], in_=a1.rearrange("(p t) n -> p t n", t=PACK))
        load_dy(1, 2)
        load_dy(1, 3)
        nc.sync.dma_start(
            out=w2_sb[:].rearrange("p e s b -> p (e s) b").bitcast(I32),
            in_=w2_words.bitcast(I32).rearrange("e s p b -> p (e s) b"),
        )
        nc.sync.dma_start(out=a3_sb[:], in_=a3.rearrange("(p t) n -> p t n", t=PACK))
        for words, tile_sb in ((w1_words, w1_sb), (w3_words, w3_sb)):
            nc.sync.dma_start(out=tile_sb[:].bitcast(I32), in_=words.bitcast(I32).rearrange("e s p b -> p (e s) b"))

        make_identity(nc, ident[:])
        nc.vector.memset(warm[:], 0.0)
        nc.scalar.activation(warm[:], warm[:], SIGMOID)
        nc.vector.memset(w2_sc[:].rearrange("p e s i -> p (e s i)").bitcast(I32), 0)
        nc.vector.memset(w1_sc[:].rearrange("p e i -> p (e i)").bitcast(I32), 0)
        nc.vector.memset(w3_sc[:].rearrange("p e i -> p (e i)").bitcast(I32), 0)
        for r in range(4):
            nc.gpsimd.dma_start(
                out=w2_sc[:].rearrange("p e s i -> p (e s) i").bitcast(I32)[r:P:32],
                in_=w2_scales.bitcast(I32).rearrange("e s (q r) i -> r q (e s) i", r=4)[r],
            )
        for scales, plane in ((w1_scales, w1_sc), (w3_scales, w3_sc)):
            for r in range(4):
                nc.gpsimd.dma_start(
                    out=plane[:].bitcast(I32)[r:P:32],
                    in_=scales.bitcast(I32).rearrange("e s (q r) i -> r q (e s) i", r=4)[r],
                )
        for k in range(K // P):
            nc.vector.memset(out_sb[k][:], 0.0)

        g = [keep.tile([P, PACK, SLOTS], F32, name=f"g{s}") for s in range(PASSES)]
        g_bf = [keep.tile([P, SLOTS, PACK], BF16, name=f"g_bf{s}", align_bytes=64) for s in range(PASSES)]
        g_codes = [keep.tile([P, SLOTS], U32, name=f"g_codes{s}", align_bytes=64) for s in range(PASSES)]
        g_sc = [keep.tile([P, SLOTS], U8, name=f"g_sc{s}", align_bytes=64) for s in range(PASSES)]
        sig = keep.tile([P, PACK, SLOTS], F32, name="sig")
        rest = [keep.tile([P, PACK, C], F32, name=f"rest{e}") for e in range(E)]
        dh = [[keep.tile([P, PACK, P], F32, name=f"dh{e}{h}") for h in range(2)] for e in range(E)]
        da3_f = [[keep.tile([P, PACK, HALF], F32, name=f"da3_f{e}{h}", align_bytes=64) for h in range(2)] for e in range(E)]
        da_bf = [keep.tile([P, 2, C, PACK], BF16, name=f"da_bf{e}", align_bytes=64) for e in range(E)]
        da_codes = [keep.tile([P, 2, C], U32, name=f"da_codes{e}", align_bytes=64) for e in range(E)]
        da_sc = [keep.tile([P, 2, C], U8, name=f"da_sc{e}", align_bytes=64) for e in range(E)]
        dx_sb = {}
        raw = {}
        turned = {}

        def gather(s, j, cols):
            lists = offsets[:, cols.start // 16 : cols.stop // 16]
            nc.vector.tensor_tensor(g[s][:, j, cols], dy[s][j][:].indirect(lists), gate_sb[:, cols], MULT)

        everything = slice(0, SLOTS)

        def side_by_side(ap):
            return ap.rearrange("p (c i) t -> p c t i", i=4)

        def apart(ap):
            return ap.rearrange("p t (c i) -> p c t i", i=4)

        def interleave(copy, s, e):
            copy(out=side_by_side(g_bf[s][:, slots(e), :]), in_=apart(g[s][:, :, slots(e)]))

        def quantize_g(s, lo, hi):
            nc.vector.quantize_mx(
                out=g_codes[s][:, lo:hi].bitcast(FP8X4),
                scales=g_sc[s][:, lo:hi],
                in_=g_bf[s][:, lo:hi, :].rearrange("p n j -> p (n j)"),
            )

        def quantize_da(e):
            nc.vector.quantize_mx(
                out=da_codes[e][:].rearrange("p w n -> p (w n)").bitcast(FP8X4),
                scales=da_sc[e][:].rearrange("p w n -> p (w n)"),
                in_=da_bf[e][:].rearrange("p w n t -> p (w n t)"),
            )

        def slots(e, h=None):
            return slice(e * C, (e + 1) * C) if h is None else slice(e * C + h * HALF, e * C + (h + 1) * HALF)

        def sigmoid(e):
            nc.scalar.activation(sig[:, :, slots(e)], a1_sb[:, :, slots(e)], SIGMOID)

        def factor(e):
            nc.vector.scalar_tensor_tensor(out=rest[e][:], in0=sig[:, :, slots(e)], scalar=1.0, in1=a3_sb[:, :, slots(e)], op0=SUBTRACT, op1=MULT)

        def first_product(e, s):
            for h in range(2):
                if s == 0:
                    raw[e, h] = raw_pool.tile([P, H], F32, name="raw_bank")
                cols = slice(e * C + h * HALF, e * C + (h + 1) * HALF)
                nc.tensor.matmul_mx(
                    out=raw[e, h][:],
                    lhsT=g_codes[s][:, cols].bitcast(FP8X4),
                    lhsT_scale=g_sc[s][:, cols],
                    rhs=w2_sb[:, e, s, :].bitcast(FP4X4),
                    rhs_scale=w2_sc[:, e, s, :],
                    start=(s == 0),
                    stop=(s == PASSES - 1),
                )

        def turn(e):
            for h in range(2):
                by_channel = raw[e, h][:].rearrange("p (m t) -> p t m", t=PACK)
                for t in range(0, PACK, 2):
                    nc.scalar.copy(out=dh[e][h][:, t : t + 2, :], in_=by_channel[:, t : t + 2, :])
            for h in range(2):
                turned[e, h] = turn_pool.tile([P, PACK, HALF], F32, name="turn_bank")
                for t in range(PACK):
                    nc.tensor.transpose(turned[e, h][:, t, :], dh[e][h][:, t, :], ident[:])

        def grad3(e, h):
            cols = slice(h * HALF, (h + 1) * HALF)
            nc.vector.tensor_tensor(da3_f[e][h][:], turned[e, h][:], sig[:, :, slots(e, h)], MULT)

        def round3(e, h):
            cols = slice(h * HALF, (h + 1) * HALF)
            nc.scalar.activation(side_by_side(da_bf[e][:, 0, cols, :]), apart(da3_f[e][h][:]), COPY, scale=-1.0)

        def grad1(engine, e, h):
            cols = slice(h * HALF, (h + 1) * HALF)
            engine.tensor_tensor(
                side_by_side(da_bf[e][:, 1, cols, :]),
                apart(da3_f[e][h][:]),
                apart(rest[e][:, :, cols]),
                MULT,
            )

        def second_product(e, k):
            bank = dx_pool.tile([P, C], F32, name="dx_bank")
            for h in range(2):
                cols = slice(h * HALF, (h + 1) * HALF)
                for i, (words, w_sc) in enumerate(((w3_sb, w3_sc), (w1_sb, w1_sc))):
                    nc.tensor.matmul_mx(
                        out=bank[:, cols],
                        lhsT=words[:, e, 2 * k * P : 2 * (k + 1) * P].bitcast(FP4X4),
                        lhsT_scale=w_sc[:, e, k * P : (k + 1) * P],
                        rhs=da_codes[e][:, i, cols].bitcast(FP8X4),
                        rhs_scale=da_sc[e][:, i, cols],
                        start=(i == 0),
                        stop=(i == 1),
                    )
            dx_sb[e, k] = keep.tile([P, C], F32, name=f"dx_sb{e}{k}")
            nc.scalar.activation(dx_sb[e, k][:], bank[:], COPY, scale=-1.0)

        def scatter(e, k):
            nc.vector.tensor_copy(out_sb[k][:].indirect(offsets[:, e * C // 16 : (e + 1) * C // 16]), dx_sb[e, k][:])

        for j in range(PACK):
            gather(0, j, everything)
        sigmoid(0)
        interleave(nc.scalar.copy, 0, 0)
        interleave(nc.scalar.copy, 0, 1)
        for j in range(PACK - 1):
            gather(1, j, everything)
        for e in range(E):
            gather(1, PACK - 1, slots(e))
        interleave(nc.scalar.copy, 1, 0)
        quantize_g(0, 0, C)
        first_product(0, 0)
        quantize_g(0, C, SLOTS)
        sigmoid(1)
        interleave(nc.scalar.copy, 1, 1)
        quantize_g(1, 0, C)
        first_product(0, 1)
        first_product(1, 0)
        factor(0)
        turn(0)
        quantize_g(1, C, SLOTS)
        first_product(1, 1)
        factor(1)
        grad3(0, 0)
        grad1(nc.gpsimd, 0, 0)
        grad3(0, 1)
        grad1(nc.vector, 0, 1)
        turn(1)
        for h in range(2):
            round3(0, h)
        quantize_da(0)
        for k in range(K // P):
            second_product(0, k)
        grad3(1, 0)
        grad1(nc.gpsimd, 1, 0)
        grad3(1, 1)
        grad1(nc.vector, 1, 1)
        for h in range(2):
            round3(1, h)
        quantize_da(1)
        for k in range(K // P):
            scatter(0, k)
        for k in range(K // P):
            second_product(1, k)
        for k in range(K // P):
            scatter(1, k)
            nc.sync.dma_start(out=out[k * P : (k + 1) * P, :], in_=out_sb[k][:])
